import numpy as np
import ml_dtypes


def mxq(x, axis, fmt="e4m3"):
    dtype, down = {"e4m3": (ml_dtypes.float8_e4m3fn, 7), "e5m2": (ml_dtypes.float8_e5m2, 14)}[fmt]
    v = np.moveaxis(np.asarray(x, np.float32).astype(ml_dtypes.bfloat16).astype(np.float64), axis, -1)
    blocks = v.reshape(v.shape[:-1] + (-1, 32))
    amax = np.abs(blocks).max(-1, keepdims=True)
    byte = np.maximum(np.where(amax > 0, np.frexp(amax)[1] - 1 + 127, 0) - down, 1)
    scale = np.exp2(byte - 127.0)
    codes = (blocks / scale).astype(np.float32).astype(dtype).astype(np.float64)
    return np.moveaxis((codes * scale).reshape(v.shape), -1, axis)


WIDE = False


def mx_kscale(k):
    if not WIDE:
        return np.ones(k)
    levels = np.array([10, -10, 5, -5, 0])
    if k % 512:
        return np.exp2(np.random.permutation(np.resize(levels, k // 32))).repeat(32)
    a = np.empty((k // 512, 16))
    for p in range(k // 512):
        a[p, :8] = np.random.permutation(np.resize(levels, 8))
        for g in range(8):
            far = levels[np.abs(levels - a[p, g]) >= 10]
            a[p, g + 8] = far[np.random.randint(len(far))]
    return np.exp2(a.ravel()).repeat(32)


def f64(x):
    return np.asarray(x).astype(np.float64)


def striped(idx):
    return np.tile(np.asarray(idx).reshape(-1, 16).T, (8, 1)).astype(np.uint16)


def unstriped(offs):
    return offs[:16].T.reshape(-1).astype(np.int64)


G, K, T, D, M = 512, 8, 2048, 512, 128


def setup_inputs():
    n = np.random.standard_normal
    s = mx_kscale(D)[:, None]
    grid = lambda x: np.round(x * 32) / 32
    x = grid(n((D, T))) * s
    idx = np.random.randint(0, T, (G, K))
    part = np.random.randint(1, 128 // K, (G, K)) / 64.0
    return {
        "xT": x.astype(np.float32),
        "w": (n((D, M)) / np.sqrt(D) / s).astype(np.float32),
        "part": np.tile(part.reshape(-1), (128, 1)).astype(np.float32),
        "bias": (0.3 * n((M, 1))).astype(np.float32),
        "offs": striped(idx.reshape(-1)),
    }


def reference(xT, w, part, bias, offs):
    x = f64(xT)[:, unstriped(offs)]
    y = mxq(f64(w), 0, "e4m3").T @ mxq((x * f64(part)[:1]).reshape(D, G, K).sum(-1), 0, "e4m3")
    y = y + f64(bias)
    y = np.maximum(y, 0.0)
    return y

@@ -1,0 +1,164 @@
+from contextlib import ExitStack
+
+import concourse.mybir as mybir
+from concourse.masks import make_identity
+
+G, J, T, D, M = 512, 8, 2048, 512, 128
+P = 128
+PACK = 4
+BLOCKS = G // P
+FLOPS = 2 * D * M * G
+BYTES = 4 * D * T + 4 * D * M + 4 * G * J + 4 * M + 2 * P * G * J // 16 + 4 * M * G
+
+F32 = mybir.dt.float32
+BF16 = mybir.dt.bfloat16
+U32 = mybir.dt.uint32
+U16 = mybir.dt.uint16
+U8 = mybir.dt.uint8
+FP8X4 = mybir.dt.float8_e4m3fn_x4
+
+COPY = mybir.ActivationFunctionType.Copy
+RELU = mybir.ActivationFunctionType.Relu
+MULT = mybir.AluOpType.mult
+ADD = mybir.AluOpType.add
+
+CHUNK = 512
+VEC_COLS = 320
+
+
+def tile_attend_grid_relu_kernel(tc, xT, w, part, bias, offs, out):
+    nc = tc.nc
+    x_rows = xT.rearrange("(p t) c -> p t c", t=PACK)
+    with ExitStack() as ctx:
+        keep = ctx.enter_context(tc.tile_pool(name="keep", bufs=1))
+        work = ctx.enter_context(tc.tile_pool(name="work", bufs=2))
+        psum = ctx.enter_context(tc.psum_pool(name="psum", bufs=1))
+
+        offsets = keep.tile([P, G * J // 16], U16, name="offsets")
+        nc.sync.dma_start(offsets[:], offs)
+        raw = {}
+        for h in range(2):
+            for c in range(T // CHUNK):
+                raw[h, c] = keep.tile([P, 2, CHUNK], F32, name="raw_%d_%d" % (h, c))
+                nc.sync.dma_start(raw[h, c][:], x_rows[:, 2 * h : 2 * h + 2, c * CHUNK : (c + 1) * CHUNK])
+        w_raw = keep.tile([P, PACK, M], F32, name="w_raw")
+        nc.sync.dma_start(w_raw[:], w.rearrange("(p t) m -> p t m", t=PACK))
+        part_cols = keep.tile([P, BLOCKS, J], F32, name="part_cols")
+        nc.scalar.dma_start(part_cols[:], part[0:1, :].rearrange("o (b g j) -> (o g) b j", b=BLOCKS, j=J))
+        bias_col = keep.tile([P, 1], F32, name="bias_col")
+        nc.scalar.dma_start(bias_col[:], bias)
+
+        identity = keep.tile([P, P], F32, name="identity")
+        make_identity(nc, identity[:])
+
+        pairs = []
+        for h in range(2):
+            pair = keep.tile([P, 2 * T], BF16, name="pair_%d" % h, align_bytes=64)
+            pairs.append(pair)
+            view = pair[:].rearrange("p (c i) -> p c i", i=2)
+            for c in range(T // CHUNK):
+                cut = VEC_COLS if h == 0 else 0
+                c0 = c * CHUNK
+                if cut:
+                    nc.vector.tensor_copy(
+                        out=view[:, c0 : c0 + cut, :], in_=raw[h, c][:, :, 0:cut].rearrange("p i c -> p c i")
+                    )
+                nc.scalar.copy(
+                    out=view[:, c0 + cut : c0 + CHUNK, :], in_=raw[h, c][:, :, cut:CHUNK].rearrange("p i c -> p c i")
+                )
+
+        def gather(h, b):
+            got = work.tile([P, 2 * P * J], BF16, name="got_%d" % h)
+            n = P * J // 16
+            nc.vector.tensor_copy(got[:].bitcast(U32), pairs[h][:].bitcast(U32).indirect(offsets[:, b * n : (b + 1) * n]))
+            return got
+
+        def turn(got_a, got_b):
+            banks = []
+            for q in range(4):
+                kind = "s" if q < 2 else "v"
+                bank = psum.tile([P, 2, 2, P], F32, name="x_" + kind, bufs=3)
+                for i in range(2):
+                    j = 2 * q + i
+                    for h, got in enumerate((got_a, got_b)):
+                        nc.tensor.transpose(bank[:, i, h, :], got[:].bitcast(F32)[:, j :: J], identity[:])
+                banks.append(bank)
+            return banks
+
+        def corner(banks, j):
+            return banks[j // 2][:, j % 2, :, :].rearrange("p h c -> p (h c)").bitcast(BF16)
+
+        def products(b, banks):
+            prods = []
+            for j in range(4):
+                prod = work.tile([P, D], F32, name="prod_%d" % j)
+                nc.scalar.activation(prod[:], corner(banks, j), COPY, scale=part_cols[:, b, j : j + 1])
+                prods.append(prod)
+            return prods
+
+        def sums(b, banks, prods):
+            halves = [work.tile([P, 2, D], F32, name="half_%d" % i) for i in range(2)]
+            for j in range(4):
+                nc.vector.scalar_tensor_tensor(
+                    halves[j // 2][:, j % 2, :], corner(banks, 4 + j), part_cols[:, b, 4 + j : 5 + j], prods[j][:], MULT, ADD
+                )
+            last = b == BLOCKS - 1
+            engine = nc.vector if last else nc.gpsimd
+            e = work.tile([P, D], BF16, name="e")
+            both = work.tile([P, 2, D], F32, name="both")
+            nc.gpsimd.tensor_tensor(both[:, 0, :], halves[0][:, 0, :], halves[0][:, 1, :], ADD)
+            engine.tensor_tensor(both[:, 1, :], halves[1][:, 0, :], halves[1][:, 1, :], ADD)
+            engine.tensor_tensor(e[:], both[:, 0, :], both[:, 1, :], ADD)
+            return e
+
+        codes = keep.tile([P, G], U32, name="codes", align_bytes=64)
+        scales = keep.tile([P, G], U8, name="scales", align_bytes=64)
+        w_codes = keep.tile([P, M], U32, name="w_codes", align_bytes=64)
+        w_scales = keep.tile([P, M], U8, name="w_scales", align_bytes=64)
+        acc = psum.tile([P, G], F32, name="acc", bufs=1)
+
+        def weights():
+            w_group = keep.tile([P, PACK * M], BF16, name="w_group", align_bytes=64)
+            nc.scalar.copy(out=w_group[:].rearrange("p (m t) -> p m t", t=PACK), in_=w_raw[:].rearrange("p t m -> p m t"))
+            nc.vector.quantize_mx(out=w_codes[:].bitcast(FP8X4), scales=w_scales[:], in_=w_group[:])
+
+        def finish(b, e):
+            back = psum.tile([P, 2, P], F32, name="back", bufs=1)
+            words = e[:].bitcast(F32)
+            for h in range(2):
+                nc.tensor.transpose(back[:, h, :], words[:, h * P : (h + 1) * P], identity[:])
+            group = work.tile([P, PACK * P], BF16, name="group", align_bytes=64)
+            nc.scalar.copy(
+                out=group[:].bitcast(F32).rearrange("p (g h) -> p g h", h=2), in_=back[:].rearrange("p h g -> p g h")
+            )
+            cols = slice(b * P, (b + 1) * P)
+            nc.vector.quantize_mx(out=codes[:, cols].bitcast(FP8X4), scales=scales[:, cols], in_=group[:])
+            nc.tensor.matmul_mx(
+                out=acc[:, cols],
+                lhsT=w_codes[:].bitcast(FP8X4),
+                lhsT_scale=w_scales[:],
+                rhs=codes[:, cols].bitcast(FP8X4),
+                rhs_scale=scales[:, cols],
+                start=True,
+                stop=True,
+            )
+            y = work.tile([P, P], F32, name="y")
+            nc.scalar.activation(y[:], acc[:, cols], RELU, bias=bias_col[:])
+            nc.sync.dma_start(out[:, cols], y[:])
+
+        got_a = {0: gather(0, 0), 1: gather(0, 1)}
+        got_b = {0: gather(1, 0)}
+        ready = {}
+        for b in range(BLOCKS):
+            banks = turn(got_a[b], got_b[b])
+            prods = products(b, banks)
+            if b + 1 < BLOCKS:
+                got_b[b + 1] = gather(1, b + 1)
+            ready[b] = sums(b, banks, prods)
+            if b == 0:
+                weights()
+            if b + 2 < BLOCKS:
+                got_a[b + 2] = gather(0, b + 2)
+            if b:
+                finish(b - 1, ready[b - 1])
+        finish(BLOCKS - 1, ready[BLOCKS - 1])

@@ -22,8 +22,11 @@ RELU = mybir.ActivationFunctionType.Relu
 MULT = mybir.AluOpType.mult
 ADD = mybir.AluOpType.add
 
-CHUNK = 512
-VEC_COLS = 320
+CHUNKS = (512, 512, 512, 256, 256)
+VEC_COLS = (512, 512, 512, 256, 256)
+UNITS = ((0, 0), (0, 1), (0, 2), (0, 3), (1, 0), (1, 1), (1, 2), (1, 3))
+FUSED = (3, 3, 3, 3, 3, 3, 3, 6)
+H = D // 2
 
 
 def tile_attend_grid_relu_kernel(tc, xT, w, part, bias, offs, out):
@@ -38,9 +41,9 @@ def tile_attend_grid_relu_kernel(tc, xT, w, part, bias, offs, out):
         nc.sync.dma_start(offsets[:], offs)
         raw = {}
         for h in range(2):
-            for c in range(T // CHUNK):
-                raw[h, c] = keep.tile([P, 2, CHUNK], F32, name="raw_%d_%d" % (h, c))
-                nc.sync.dma_start(raw[h, c][:], x_rows[:, 2 * h : 2 * h + 2, c * CHUNK : (c + 1) * CHUNK])
+            for c, width in enumerate(CHUNKS):
+                raw[h, c] = keep.tile([P, 2, width], F32, name="raw_%d_%d" % (h, c))
+                nc.sync.dma_start(raw[h, c][:], x_rows[:, 2 * h : 2 * h + 2, sum(CHUNKS[:c]) : sum(CHUNKS[: c + 1])])
         w_raw = keep.tile([P, PACK, M], F32, name="w_raw")
         nc.sync.dma_start(w_raw[:], w.rearrange("(p t) m -> p t m", t=PACK))
         part_cols = keep.tile([P, BLOCKS, J], F32, name="part_cols")
@@ -56,60 +59,71 @@ def tile_attend_grid_relu_kernel(tc, xT, w, part, bias, offs, out):
             pair = keep.tile([P, 2 * T], BF16, name="pair_%d" % h, align_bytes=64)
             pairs.append(pair)
             view = pair[:].rearrange("p (c i) -> p c i", i=2)
-            for c in range(T // CHUNK):
-                cut = VEC_COLS if h == 0 else 0
-                c0 = c * CHUNK
+            for c, width in enumerate(CHUNKS):
+                cut = VEC_COLS[c] if h == 0 else 0
+                c0 = sum(CHUNKS[:c])
                 if cut:
                     nc.vector.tensor_copy(
                         out=view[:, c0 : c0 + cut, :], in_=raw[h, c][:, :, 0:cut].rearrange("p i c -> p c i")
                     )
-                nc.scalar.copy(
-                    out=view[:, c0 + cut : c0 + CHUNK, :], in_=raw[h, c][:, :, cut:CHUNK].rearrange("p i c -> p c i")
-                )
+                if cut < width:
+                    nc.scalar.copy(
+                        out=view[:, c0 + cut : c0 + width, :], in_=raw[h, c][:, :, cut:width].rearrange("p i c -> p c i")
+                    )
 
         def gather(h, b):
-            got = work.tile([P, 2 * P * J], BF16, name="got_%d" % h)
+            unit = work.tile([P, J * P + H], F32, name="unit", bufs=2)
             n = P * J // 16
-            nc.vector.tensor_copy(got[:].bitcast(U32), pairs[h][:].bitcast(U32).indirect(offsets[:, b * n : (b + 1) * n]))
-            return got
+            nc.vector.tensor_copy(
+                unit[:, 0 : J * P].bitcast(U32), pairs[h][:].bitcast(U32).indirect(offsets[:, b * n : (b + 1) * n])
+            )
+            return unit
 
-        def turn(got_a, got_b):
-            banks = []
-            for q in range(4):
-                kind = "s" if q < 2 else "v"
-                bank = psum.tile([P, 2, 2, P], F32, name="x_" + kind, bufs=3)
-                for i in range(2):
-                    j = 2 * q + i
-                    for h, got in enumerate((got_a, got_b)):
-                        nc.tensor.transpose(bank[:, i, h, :], got[:].bitcast(F32)[:, j :: J], identity[:])
-                banks.append(bank)
-            return banks
+        def turn(u, unit):
+            groups = ((0, 3, "s"), (3, 5, "s"), (5, 8, "v")) if FUSED[u] == 3 else ((0, 2, "s"), (2, 5, "s"), (5, 8, "v"))
+            where = []
+            for j0, j1, kind in groups:
+                bank = psum.tile([P, 4, P], F32, name="x_" + kind, bufs=4 if kind == "s" else 1)
+                for j in range(j0, j1):
+                    nc.tensor.transpose(bank[:, j - j0, :], unit[:, j : J * P : J], identity[:])
+                    where.append(bank[:, j - j0, :].bitcast(BF16))
+            return where
 
-        def corner(banks, j):
-            return banks[j // 2][:, j % 2, :, :].rearrange("p h c -> p (h c)").bitcast(BF16)
-
-        def products(b, banks):
-            prods = []
-            for j in range(4):
-                prod = work.tile([P, D], F32, name="prod_%d" % j)
-                nc.scalar.activation(prod[:], corner(banks, j), COPY, scale=part_cols[:, b, j : j + 1])
-                prods.append(prod)
+        def products(u, where):
+            b = UNITS[u][1]
+            prods = work.tile([P, J - 3, H], F32, name="prods", bufs=3)
+            for j in range(J - FUSED[u]):
+                nc.scalar.activation(prods[:, j, :], where[j], COPY, scale=part_cols[:, b, j : j + 1])
             return prods
 
-        def sums(b, banks, prods):
-            halves = [work.tile([P, 2, D], F32, name="half_%d" % i) for i in range(2)]
-            for j in range(4):
-                nc.vector.scalar_tensor_tensor(
-                    halves[j // 2][:, j % 2, :], corner(banks, 4 + j), part_cols[:, b, 4 + j : 5 + j], prods[j][:], MULT, ADD
-                )
-            last = b == BLOCKS - 1
-            engine = nc.vector if last else nc.gpsimd
-            e = work.tile([P, D], BF16, name="e")
-            both = work.tile([P, 2, D], F32, name="both")
-            nc.gpsimd.tensor_tensor(both[:, 0, :], halves[0][:, 0, :], halves[0][:, 1, :], ADD)
-            engine.tensor_tensor(both[:, 1, :], halves[1][:, 0, :], halves[1][:, 1, :], ADD)
-            engine.tensor_tensor(e[:], both[:, 0, :], both[:, 1, :], ADD)
-            return e
+        def sums(u, where, prods, unit, e):
+            b = UNITS[u][1]
+            first = J - FUSED[u]
+
+            def fuse(out, j, other):
+                nc.vector.scalar_tensor_tensor(out, where[j], part_cols[:, b, j : j + 1], other, MULT, ADD)
+
+            private = unit[:, J * P : J * P + H]
+            fused = work.tile([P, 2, H], F32, name="fused", bufs=3)
+            if FUSED[u] == 3:
+                fuse(private, 5, prods[:, 0, :])
+                fuse(fused[:, 0, :], 6, prods[:, 1, :])
+                fuse(fused[:, 1, :], 7, private)
+                two = work.tile([P, 2, H], F32, name="two")
+                one = work.tile([P, H], F32, name="one")
+                nc.gpsimd.tensor_tensor(two[:], fused[:], prods[:, 2:4, :], ADD)
+                nc.gpsimd.tensor_tensor(one[:], two[:, 0, :], two[:, 1, :], ADD)
+                nc.gpsimd.tensor_tensor(e, one[:], prods[:, 4, :], ADD)
+            else:
+                fuse(private, 2, prods[:, 0, :])
+                fuse(fused[:, 0, :], 3, prods[:, 1, :])
+                more = work.tile([P, 2, H], F32, name="more")
+                fuse(more[:, 0, :], 4, private)
+                fuse(more[:, 1, :], 5, fused[:, 0, :])
+                ends = work.tile([P, 2, H], F32, name="ends")
+                fuse(ends[:, 0, :], 6, more[:, 0, :])
+                fuse(ends[:, 1, :], 7, more[:, 1, :])
+                nc.vector.tensor_tensor(e, ends[:, 0, :], ends[:, 1, :], ADD)
 
         codes = keep.tile([P, G], U32, name="codes", align_bytes=64)
         scales = keep.tile([P, G], U8, name="scales", align_bytes=64)
@@ -122,9 +136,9 @@ def tile_attend_grid_relu_kernel(tc, xT, w, part, bias, offs, out):
             nc.scalar.copy(out=w_group[:].rearrange("p (m t) -> p m t", t=PACK), in_=w_raw[:].rearrange("p t m -> p m t"))
             nc.vector.quantize_mx(out=w_codes[:].bitcast(FP8X4), scales=w_scales[:], in_=w_group[:])
 
-        def finish(b, e):
+        def finish(b):
             back = psum.tile([P, 2, P], F32, name="back", bufs=1)
-            words = e[:].bitcast(F32)
+            words = e_blocks[b][:].bitcast(F32)
             for h in range(2):
                 nc.tensor.transpose(back[:, h, :], words[:, h * P : (h + 1) * P], identity[:])
             group = work.tile([P, PACK * P], BF16, name="group", align_bytes=64)
@@ -146,19 +160,24 @@ def tile_attend_grid_relu_kernel(tc, xT, w, part, bias, offs, out):
             nc.scalar.activation(y[:], acc[:, cols], RELU, bias=bias_col[:])
             nc.sync.dma_start(out[:, cols], y[:])
 
-        got_a = {0: gather(0, 0), 1: gather(0, 1)}
-        got_b = {0: gather(1, 0)}
-        ready = {}
-        for b in range(BLOCKS):
-            banks = turn(got_a[b], got_b[b])
-            prods = products(b, banks)
-            if b + 1 < BLOCKS:
-                got_b[b + 1] = gather(1, b + 1)
-            ready[b] = sums(b, banks, prods)
-            if b == 0:
+        e_blocks = [keep.tile([P, D], BF16, name="e_%d" % b) for b in range(BLOCKS)]
+        ahead = gather(*UNITS[0])
+        done = []
+        pending = []
+        for u, (h, b) in enumerate(UNITS):
+            unit = ahead
+            where = turn(u, unit)
+            prods = products(u, where)
+            if u + 1 < len(UNITS):
+                ahead = gather(*UNITS[u + 1])
+            sums(u, where, prods, unit, e_blocks[b][:, h * H : (h + 1) * H])
+            if u == 3:
                 weights()
-            if b + 2 < BLOCKS:
-                got_a[b + 2] = gather(0, b + 2)
-            if b:
-                finish(b - 1, ready[b - 1])
-        finish(BLOCKS - 1, ready[BLOCKS - 1])
+            for ready in pending:
+                finish(ready)
+            pending = []
+            done.append(b)
+            if done.count(b) == 2:
+                pending.append(b)
+        for ready in pending:
+            finish(ready)

@@ -25,7 +25,7 @@ ADD = mybir.AluOpType.add
 CHUNKS = (512, 512, 512, 256, 256)
 VEC_COLS = (512, 512, 512, 256, 256)
 UNITS = ((0, 0), (0, 1), (0, 2), (0, 3), (1, 0), (1, 1), (1, 2), (1, 3))
-FUSED = (3, 3, 3, 3, 3, 3, 3, 6)
+FUSED = (3, 3, 3, 3, 3, 3, 3, 5)
 H = D // 2
 
 
@@ -38,10 +38,11 @@ def tile_attend_grid_relu_kernel(tc, xT, w, part, bias, offs, out):
         psum = ctx.enter_context(tc.psum_pool(name="psum", bufs=1))
 
         offsets = keep.tile([P, G * J // 16], U16, name="offsets")
-        nc.sync.dma_start(offsets[:], offs)
         raw = {}
         for h in range(2):
             for c, width in enumerate(CHUNKS):
+                if h == 0 and c == len(CHUNKS) - 1:
+                    nc.sync.dma_start(offsets[:], offs)
                 raw[h, c] = keep.tile([P, 2, width], F32, name="raw_%d_%d" % (h, c))
                 nc.sync.dma_start(raw[h, c][:], x_rows[:, 2 * h : 2 * h + 2, sum(CHUNKS[:c]) : sum(CHUNKS[: c + 1])])
         w_raw = keep.tile([P, PACK, M], F32, name="w_raw")
@@ -72,26 +73,30 @@ def tile_attend_grid_relu_kernel(tc, xT, w, part, bias, offs, out):
                     )
 
         def gather(h, b):
-            unit = work.tile([P, J * P + H], F32, name="unit", bufs=2)
+            unit = work.tile([P, J * P + H], F32, name="unit", bufs=3)
             n = P * J // 16
             nc.vector.tensor_copy(
-                unit[:, 0 : J * P].bitcast(U32), pairs[h][:].bitcast(U32).indirect(offsets[:, b * n : (b + 1) * n])
+                unit[:, 0 : J * P].bitcast(U32).rearrange("p (q g i) -> p g q i", q=4, i=2), pairs[h][:].bitcast(U32).indirect(offsets[:, b * n : (b + 1) * n])
             )
             return unit
 
         def turn(u, unit):
-            groups = ((0, 3, "s"), (3, 5, "s"), (5, 8, "v")) if FUSED[u] == 3 else ((0, 2, "s"), (2, 5, "s"), (5, 8, "v"))
+            groups = {
+                2: ((0, 3, "s"), (3, 6, "s"), (6, 8, "v")),
+                3: ((0, 3, "s"), (3, 5, "s"), (5, 8, "v")),
+                5: ((0, 3, "s"), (3, 5, "s"), (5, 8, "v")),
+            }[FUSED[u]]
             where = []
             for j0, j1, kind in groups:
-                bank = psum.tile([P, 4, P], F32, name="x_" + kind, bufs=4 if kind == "s" else 1)
+                bank = psum.tile([P, 4, P], F32, name="x_" + kind, bufs=4 if kind == "s" else 3)
                 for j in range(j0, j1):
-                    nc.tensor.transpose(bank[:, j - j0, :], unit[:, j : J * P : J], identity[:])
+                    nc.tensor.transpose(bank[:, j - j0, :], unit[:, j // 2 * 2 * P + j % 2 : (j // 2 + 1) * 2 * P : 2], identity[:])
                     where.append(bank[:, j - j0, :].bitcast(BF16))
             return where
 
         def products(u, where):
             b = UNITS[u][1]
-            prods = work.tile([P, J - 3, H], F32, name="prods", bufs=3)
+            prods = work.tile([P, J - 2, H], F32, name="prods", bufs=3)
             for j in range(J - FUSED[u]):
                 nc.scalar.activation(prods[:, j, :], where[j], COPY, scale=part_cols[:, b, j : j + 1])
             return prods
@@ -105,50 +110,65 @@ def tile_attend_grid_relu_kernel(tc, xT, w, part, bias, offs, out):
 
             private = unit[:, J * P : J * P + H]
             fused = work.tile([P, 2, H], F32, name="fused", bufs=3)
-            if FUSED[u] == 3:
-                fuse(private, 5, prods[:, 0, :])
-                fuse(fused[:, 0, :], 6, prods[:, 1, :])
-                fuse(fused[:, 1, :], 7, private)
-                two = work.tile([P, 2, H], F32, name="two")
-                one = work.tile([P, H], F32, name="one")
-                nc.gpsimd.tensor_tensor(two[:], fused[:], prods[:, 2:4, :], ADD)
+            if FUSED[u] == 2:
+                two = work.tile([P, 2, H], F32, name="two", bufs=3)
+                nc.gpsimd.tensor_tensor(two[:], prods[:, 0:2, :], prods[:, 2:4, :], ADD)
+                one = work.tile([P, H], F32, name="one", bufs=3)
                 nc.gpsimd.tensor_tensor(one[:], two[:, 0, :], two[:, 1, :], ADD)
-                nc.gpsimd.tensor_tensor(e, one[:], prods[:, 4, :], ADD)
+                more = work.tile([P, H], F32, name="more_one", bufs=3)
+                nc.gpsimd.tensor_tensor(more[:], one[:], prods[:, 5, :], ADD)
+                fuse(private, 6, prods[:, 4, :])
+                fuse(fused[:, 0, :], 7, private)
+                nc.gpsimd.tensor_tensor(e, fused[:, 0, :], more[:], ADD)
+            elif FUSED[u] == 3:
+                two = work.tile([P, 2, H], F32, name="two", bufs=3)
+                nc.gpsimd.tensor_tensor(two[:], prods[:, 0:2, :], prods[:, 2:4, :], ADD)
+                one = work.tile([P, H], F32, name="one", bufs=3)
+                nc.gpsimd.tensor_tensor(one[:], two[:, 0, :], two[:, 1, :], ADD)
+                fuse(private, 5, prods[:, 4, :])
+                fuse(fused[:, 0, :], 6, one[:])
+                fuse(fused[:, 1, :], 7, private)
+                nc.gpsimd.tensor_tensor(e, fused[:, 0, :], fused[:, 1, :], ADD)
             else:
-                fuse(private, 2, prods[:, 0, :])
-                fuse(fused[:, 0, :], 3, prods[:, 1, :])
+                one = work.tile([P, H], F32, name="one", bufs=3)
+                nc.gpsimd.tensor_tensor(one[:], prods[:, 0, :], prods[:, 1, :], ADD)
+                fuse(private, 3, prods[:, 2, :])
+                fuse(fused[:, 0, :], 4, one[:])
                 more = work.tile([P, 2, H], F32, name="more")
-                fuse(more[:, 0, :], 4, private)
-                fuse(more[:, 1, :], 5, fused[:, 0, :])
-                ends = work.tile([P, 2, H], F32, name="ends")
-                fuse(ends[:, 0, :], 6, more[:, 0, :])
-                fuse(ends[:, 1, :], 7, more[:, 1, :])
-                nc.vector.tensor_tensor(e, ends[:, 0, :], ends[:, 1, :], ADD)
+                fuse(more[:, 0, :], 5, private)
+                fuse(more[:, 1, :], 6, fused[:, 0, :])
+                end = work.tile([P, H], F32, name="end")
+                fuse(end[:], 7, more[:, 0, :])
+                nc.vector.tensor_tensor(e, end[:], more[:, 1, :], ADD)
 
         codes = keep.tile([P, G], U32, name="codes", align_bytes=64)
         scales = keep.tile([P, G], U8, name="scales", align_bytes=64)
         w_codes = keep.tile([P, M], U32, name="w_codes", align_bytes=64)
         w_scales = keep.tile([P, M], U8, name="w_scales", align_bytes=64)
-        acc = psum.tile([P, G], F32, name="acc", bufs=1)
 
         def weights():
             w_group = keep.tile([P, PACK * M], BF16, name="w_group", align_bytes=64)
             nc.scalar.copy(out=w_group[:].rearrange("p (m t) -> p m t", t=PACK), in_=w_raw[:].rearrange("p t m -> p m t"))
             nc.vector.quantize_mx(out=w_codes[:].bitcast(FP8X4), scales=w_scales[:], in_=w_group[:])
 
-        def finish(b):
-            back = psum.tile([P, 2, P], F32, name="back", bufs=1)
-            words = e_blocks[b][:].bitcast(F32)
-            for h in range(2):
-                nc.tensor.transpose(back[:, h, :], words[:, h * P : (h + 1) * P], identity[:])
-            group = work.tile([P, PACK * P], BF16, name="group", align_bytes=64)
-            nc.scalar.copy(
-                out=group[:].bitcast(F32).rearrange("p (g h) -> p g h", h=2), in_=back[:].rearrange("p h g -> p g h")
-            )
-            cols = slice(b * P, (b + 1) * P)
-            nc.vector.quantize_mx(out=codes[:, cols].bitcast(FP8X4), scales=scales[:, cols], in_=group[:])
+        def finish(blocks):
+            n = len(blocks) * P
+            group = work.tile([P, 2 * PACK * P], BF16, name="group", bufs=3, align_bytes=64)
+            for i, b in enumerate(blocks):
+                back = psum.tile([P, 4, P], F32, name="x_s", bufs=4)
+                words = e_blocks[b][:].bitcast(F32)
+                for h in range(2):
+                    nc.tensor.transpose(back[:, h, :], words[:, h * P : (h + 1) * P], identity[:])
+                nc.scalar.copy(
+                    out=group[:, i * PACK * P : (i + 1) * PACK * P].bitcast(F32).rearrange("p (g h) -> p g h", h=2),
+                    in_=back[:, 0:2, :].rearrange("p h g -> p g h"),
+                )
+            cols = slice(blocks[0] * P, blocks[0] * P + n)
+            nc.vector.quantize_mx(out=codes[:, cols].bitcast(FP8X4), scales=scales[:, cols], in_=group[:, 0 : PACK * n])
+            acc = psum.tile([P, 4, P], F32, name="x_v", bufs=3)
+            sums_mx = acc[:, 0 : len(blocks), :].rearrange("p b g -> p (b g)")
             nc.tensor.matmul_mx(
-                out=acc[:, cols],
+                out=sums_mx,
                 lhsT=w_codes[:].bitcast(FP8X4),
                 lhsT_scale=w_scales[:],
                 rhs=codes[:, cols].bitcast(FP8X4),
@@ -156,28 +176,21 @@ def tile_attend_grid_relu_kernel(tc, xT, w, part, bias, offs, out):
                 start=True,
                 stop=True,
             )
-            y = work.tile([P, P], F32, name="y")
-            nc.scalar.activation(y[:], acc[:, cols], RELU, bias=bias_col[:])
-            nc.sync.dma_start(out[:, cols], y[:])
+            y = work.tile([P, 2 * P], F32, name="y", bufs=3)
+            nc.scalar.activation(y[:, 0:n], sums_mx, RELU, bias=bias_col[:])
+            nc.sync.dma_start(out[:, cols], y[:, 0:n])
 
         e_blocks = [keep.tile([P, D], BF16, name="e_%d" % b) for b in range(BLOCKS)]
-        ahead = gather(*UNITS[0])
-        done = []
-        pending = []
+        ahead = [gather(*UNITS[u]) for u in range(2)]
         for u, (h, b) in enumerate(UNITS):
-            unit = ahead
+            unit = ahead[u]
             where = turn(u, unit)
             prods = products(u, where)
-            if u + 1 < len(UNITS):
-                ahead = gather(*UNITS[u + 1])
+            if u + 2 < len(UNITS):
+                ahead.append(gather(*UNITS[u + 2]))
             sums(u, where, prods, unit, e_blocks[b][:, h * H : (h + 1) * H])
             if u == 3:
                 weights()
-            for ready in pending:
-                finish(ready)
-            pending = []
-            done.append(b)
-            if done.count(b) == 2:
-                pending.append(b)
-        for ready in pending:
-            finish(ready)
+        finish((0, 1))
+        finish((2,))
+        finish((3,))

@@ -50,7 +50,7 @@ def tile_attend_grid_relu_kernel(tc, xT, w, part, bias, offs, out):
         part_cols = keep.tile([P, BLOCKS, J], F32, name="part_cols")
         nc.scalar.dma_start(part_cols[:], part[0:1, :].rearrange("o (b g j) -> (o g) b j", b=BLOCKS, j=J))
         bias_col = keep.tile([P, 1], F32, name="bias_col")
-        nc.scalar.dma_start(bias_col[:], bias)
+        nc.sync.dma_start(bias_col[:], bias)
 
         identity = keep.tile([P, P], F32, name="identity")
         make_identity(nc, identity[:])
@@ -110,7 +110,17 @@ def tile_attend_grid_relu_kernel(tc, xT, w, part, bias, offs, out):
 
             private = unit[:, J * P : J * P + H]
             fused = work.tile([P, 2, H], F32, name="fused", bufs=3)
-            if FUSED[u] == 2:
+            if u == 0:
+                early = work.tile([P, 2, H], F32, name="early")
+                nc.gpsimd.tensor_tensor(early[:, 0, :], prods[:, 0, :], prods[:, 1, :], ADD)
+                nc.gpsimd.tensor_tensor(early[:, 1, :], early[:, 0, :], prods[:, 2, :], ADD)
+                fuse(private, 5, prods[:, 3, :])
+                fuse(fused[:, 0, :], 6, prods[:, 4, :])
+                fuse(fused[:, 1, :], 7, private)
+                one = work.tile([P, H], F32, name="one", bufs=3)
+                nc.gpsimd.tensor_tensor(one[:], fused[:, 0, :], fused[:, 1, :], ADD)
+                nc.gpsimd.tensor_tensor(e, one[:], early[:, 1, :], ADD)
+            elif FUSED[u] == 2:
                 two = work.tile([P, 2, H], F32, name="two", bufs=3)
                 nc.gpsimd.tensor_tensor(two[:], prods[:, 0:2, :], prods[:, 2:4, :], ADD)
                 one = work.tile([P, H], F32, name="one", bufs=3)

from contextlib import ExitStack

import concourse.mybir as mybir
from concourse.masks import make_identity

G, J, T, D, M = 512, 8, 2048, 512, 128
P = 128
PACK = 4
BLOCKS = G // P
FLOPS = 2 * D * M * G
BYTES = 4 * D * T + 4 * D * M + 4 * G * J + 4 * M + 2 * P * G * J // 16 + 4 * M * G

F32 = mybir.dt.float32
BF16 = mybir.dt.bfloat16
U32 = mybir.dt.uint32
U16 = mybir.dt.uint16
U8 = mybir.dt.uint8
FP8X4 = mybir.dt.float8_e4m3fn_x4

COPY = mybir.ActivationFunctionType.Copy
RELU = mybir.ActivationFunctionType.Relu
MULT = mybir.AluOpType.mult
ADD = mybir.AluOpType.add

CHUNKS = (512, 512, 512, 256, 256)
VEC_COLS = (512, 512, 512, 256, 256)
UNITS = ((0, 0), (0, 1), (0, 2), (0, 3), (1, 0), (1, 1), (1, 2), (1, 3))
FUSED = (3, 3, 3, 3, 3, 3, 3, 5)
H = D // 2


def tile_attend_grid_relu_kernel(tc, xT, w, part, bias, offs, out):
    nc = tc.nc
    x_rows = xT.rearrange("(p t) c -> p t c", t=PACK)
    with ExitStack() as ctx:
        keep = ctx.enter_context(tc.tile_pool(name="keep", bufs=1))
        work = ctx.enter_context(tc.tile_pool(name="work", bufs=2))
        psum = ctx.enter_context(tc.psum_pool(name="psum", bufs=1))

        offsets = keep.tile([P, G * J // 16], U16, name="offsets")
        raw = {}
        for h in range(2):
            for c, width in enumerate(CHUNKS):
                if h == 0 and c == len(CHUNKS) - 1:
                    nc.sync.dma_start(offsets[:], offs)
                raw[h, c] = keep.tile([P, 2, width], F32, name="raw_%d_%d" % (h, c))
                nc.sync.dma_start(raw[h, c][:], x_rows[:, 2 * h : 2 * h + 2, sum(CHUNKS[:c]) : sum(CHUNKS[: c + 1])])
        w_raw = keep.tile([P, PACK, M], F32, name="w_raw")
        nc.sync.dma_start(w_raw[:], w.rearrange("(p t) m -> p t m", t=PACK))
        part_cols = keep.tile([P, BLOCKS, J], F32, name="part_cols")
        nc.scalar.dma_start(part_cols[:], part[0:1, :].rearrange("o (b g j) -> (o g) b j", b=BLOCKS, j=J))
        bias_col = keep.tile([P, 1], F32, name="bias_col")
        nc.sync.dma_start(bias_col[:], bias)

        identity = keep.tile([P, P], F32, name="identity")
        make_identity(nc, identity[:])

        pairs = []
        for h in range(2):
            pair = keep.tile([P, 2 * T], BF16, name="pair_%d" % h, align_bytes=64)
            pairs.append(pair)
            view = pair[:].rearrange("p (c i) -> p c i", i=2)
            for c, width in enumerate(CHUNKS):
                cut = VEC_COLS[c] if h == 0 else 0
                c0 = sum(CHUNKS[:c])
                if cut:
                    nc.vector.tensor_copy(
                        out=view[:, c0 : c0 + cut, :], in_=raw[h, c][:, :, 0:cut].rearrange("p i c -> p c i")
                    )
                if cut < width:
                    nc.scalar.copy(
                        out=view[:, c0 + cut : c0 + width, :], in_=raw[h, c][:, :, cut:width].rearrange("p i c -> p c i")
                    )

        def gather(h, b):
            unit = work.tile([P, J * P + H], F32, name="unit", bufs=3)
            n = P * J // 16
            nc.vector.tensor_copy(
                unit[:, 0 : J * P].bitcast(U32).rearrange("p (q g i) -> p g q i", q=4, i=2), pairs[h][:].bitcast(U32).indirect(offsets[:, b * n : (b + 1) * n])
            )
            return unit

        def turn(u, unit):
            groups = {
                2: ((0, 3, "s"), (3, 6, "s"), (6, 8, "v")),
                3: ((0, 3, "s"), (3, 5, "s"), (5, 8, "v")),
                5: ((0, 3, "s"), (3, 5, "s"), (5, 8, "v")),
            }[FUSED[u]]
            where = []
            for j0, j1, kind in groups:
                bank = psum.tile([P, 4, P], F32, name="x_" + kind, bufs=4 if kind == "s" else 3)
                for j in range(j0, j1):
                    nc.tensor.transpose(bank[:, j - j0, :], unit[:, j // 2 * 2 * P + j % 2 : (j // 2 + 1) * 2 * P : 2], identity[:])
                    where.append(bank[:, j - j0, :].bitcast(BF16))
            return where

        def products(u, where):
            b = UNITS[u][1]
            prods = work.tile([P, J - 2, H], F32, name="prods", bufs=3)
            for j in range(J - FUSED[u]):
                nc.scalar.activation(prods[:, j, :], where[j], COPY, scale=part_cols[:, b, j : j + 1])
            return prods

        def sums(u, where, prods, unit, e):
            b = UNITS[u][1]
            first = J - FUSED[u]

            def fuse(out, j, other):
                nc.vector.scalar_tensor_tensor(out, where[j], part_cols[:, b, j : j + 1], other, MULT, ADD)

            private = unit[:, J * P : J * P + H]
            fused = work.tile([P, 2, H], F32, name="fused", bufs=3)
            if u == 0:
                early = work.tile([P, 2, H], F32, name="early")
                nc.gpsimd.tensor_tensor(early[:, 0, :], prods[:, 0, :], prods[:, 1, :], ADD)
                nc.gpsimd.tensor_tensor(early[:, 1, :], early[:, 0, :], prods[:, 2, :], ADD)
                fuse(private, 5, prods[:, 3, :])
                fuse(fused[:, 0, :], 6, prods[:, 4, :])
                fuse(fused[:, 1, :], 7, private)
                one = work.tile([P, H], F32, name="one", bufs=3)
                nc.gpsimd.tensor_tensor(one[:], fused[:, 0, :], fused[:, 1, :], ADD)
                nc.gpsimd.tensor_tensor(e, one[:], early[:, 1, :], ADD)
            elif FUSED[u] == 2:
                two = work.tile([P, 2, H], F32, name="two", bufs=3)
                nc.gpsimd.tensor_tensor(two[:], prods[:, 0:2, :], prods[:, 2:4, :], ADD)
                one = work.tile([P, H], F32, name="one", bufs=3)
                nc.gpsimd.tensor_tensor(one[:], two[:, 0, :], two[:, 1, :], ADD)
                more = work.tile([P, H], F32, name="more_one", bufs=3)
                nc.gpsimd.tensor_tensor(more[:], one[:], prods[:, 5, :], ADD)
                fuse(private, 6, prods[:, 4, :])
                fuse(fused[:, 0, :], 7, private)
                nc.gpsimd.tensor_tensor(e, fused[:, 0, :], more[:], ADD)
            elif FUSED[u] == 3:
                two = work.tile([P, 2, H], F32, name="two", bufs=3)
                nc.gpsimd.tensor_tensor(two[:], prods[:, 0:2, :], prods[:, 2:4, :], ADD)
                one = work.tile([P, H], F32, name="one", bufs=3)
                nc.gpsimd.tensor_tensor(one[:], two[:, 0, :], two[:, 1, :], ADD)
                fuse(private, 5, prods[:, 4, :])
                fuse(fused[:, 0, :], 6, one[:])
                fuse(fused[:, 1, :], 7, private)
                nc.gpsimd.tensor_tensor(e, fused[:, 0, :], fused[:, 1, :], ADD)
            else:
                one = work.tile([P, H], F32, name="one", bufs=3)
                nc.gpsimd.tensor_tensor(one[:], prods[:, 0, :], prods[:, 1, :], ADD)
                fuse(private, 3, prods[:, 2, :])
                fuse(fused[:, 0, :], 4, one[:])
                more = work.tile([P, 2, H], F32, name="more")
                fuse(more[:, 0, :], 5, private)
                fuse(more[:, 1, :], 6, fused[:, 0, :])
                end = work.tile([P, H], F32, name="end")
                fuse(end[:], 7, more[:, 0, :])
                nc.vector.tensor_tensor(e, end[:], more[:, 1, :], ADD)

        codes = keep.tile([P, G], U32, name="codes", align_bytes=64)
        scales = keep.tile([P, G], U8, name="scales", align_bytes=64)
        w_codes = keep.tile([P, M], U32, name="w_codes", align_bytes=64)
        w_scales = keep.tile([P, M], U8, name="w_scales", align_bytes=64)

        def weights():
            w_group = keep.tile([P, PACK * M], BF16, name="w_group", align_bytes=64)
            nc.scalar.copy(out=w_group[:].rearrange("p (m t) -> p m t", t=PACK), in_=w_raw[:].rearrange("p t m -> p m t"))
            nc.vector.quantize_mx(out=w_codes[:].bitcast(FP8X4), scales=w_scales[:], in_=w_group[:])

        def finish(blocks):
            n = len(blocks) * P
            group = work.tile([P, 2 * PACK * P], BF16, name="group", bufs=3, align_bytes=64)
            for i, b in enumerate(blocks):
                back = psum.tile([P, 4, P], F32, name="x_s", bufs=4)
                words = e_blocks[b][:].bitcast(F32)
                for h in range(2):
                    nc.tensor.transpose(back[:, h, :], words[:, h * P : (h + 1) * P], identity[:])
                nc.scalar.copy(
                    out=group[:, i * PACK * P : (i + 1) * PACK * P].bitcast(F32).rearrange("p (g h) -> p g h", h=2),
                    in_=back[:, 0:2, :].rearrange("p h g -> p g h"),
                )
            cols = slice(blocks[0] * P, blocks[0] * P + n)
            nc.vector.quantize_mx(out=codes[:, cols].bitcast(FP8X4), scales=scales[:, cols], in_=group[:, 0 : PACK * n])
            acc = psum.tile([P, 4, P], F32, name="x_v", bufs=3)
            sums_mx = acc[:, 0 : len(blocks), :].rearrange("p b g -> p (b g)")
            nc.tensor.matmul_mx(
                out=sums_mx,
                lhsT=w_codes[:].bitcast(FP8X4),
                lhsT_scale=w_scales[:],
                rhs=codes[:, cols].bitcast(FP8X4),
                rhs_scale=scales[:, cols],
                start=True,
                stop=True,
            )
            y = work.tile([P, 2 * P], F32, name="y", bufs=3)
            nc.scalar.activation(y[:, 0:n], sums_mx, RELU, bias=bias_col[:])
            nc.sync.dma_start(out[:, cols], y[:, 0:n])

        e_blocks = [keep.tile([P, D], BF16, name="e_%d" % b) for b in range(BLOCKS)]
        ahead = [gather(*UNITS[u]) for u in range(2)]
        for u, (h, b) in enumerate(UNITS):
            unit = ahead[u]
            where = turn(u, unit)
            prods = products(u, where)
            if u + 2 < len(UNITS):
                ahead.append(gather(*UNITS[u + 2]))
            sums(u, where, prods, unit, e_blocks[b][:, h * H : (h + 1) * H])
            if u == 3:
                weights()
        finish((0, 1))
        finish((2,))
        finish((3,))
